import numpy as np
import ml_dtypes


def mxq(x, axis, fmt="e4m3"):
    dtype, down = {"e4m3": (ml_dtypes.float8_e4m3fn, 7), "e5m2": (ml_dtypes.float8_e5m2, 14)}[fmt]
    v = np.moveaxis(np.asarray(x, np.float32).astype(ml_dtypes.bfloat16).astype(np.float64), axis, -1)
    blocks = v.reshape(v.shape[:-1] + (-1, 32))
    amax = np.abs(blocks).max(-1, keepdims=True)
    byte = np.maximum(np.where(amax > 0, np.frexp(amax)[1] - 1 + 127, 0) - down, 1)
    scale = np.exp2(byte - 127.0)
    codes = (blocks / scale).astype(np.float32).astype(dtype).astype(np.float64)
    return np.moveaxis((codes * scale).reshape(v.shape), -1, axis)


WIDE = False


def mx_kscale(k):
    if not WIDE:
        return np.ones(k)
    levels = np.array([10, -10, 5, -5, 0])
    if k % 512:
        return np.exp2(np.random.permutation(np.resize(levels, k // 32))).repeat(32)
    a = np.empty((k // 512, 16))
    for p in range(k // 512):
        a[p, :8] = np.random.permutation(np.resize(levels, 8))
        for g in range(8):
            far = levels[np.abs(levels - a[p, g]) >= 10]
            a[p, g + 8] = far[np.random.randint(len(far))]
    return np.exp2(a.ravel()).repeat(32)


def f64(x):
    return np.asarray(x).astype(np.float64)


def striped(idx):
    return np.tile(idx.reshape(-1, 16).T, (8, 1)).astype(np.uint16)


def unstriped(offs):
    return offs[:16].T.reshape(-1).astype(np.int64)


E2M1 = np.array([0.0, 0.5, 1.0, 1.5, 2.0, 3.0, 4.0, 6.0, -0.0, -0.5, -1.0, -1.5, -2.0, -3.0, -4.0, -6.0])


def pack_weight(w, fmt):
    k, n = w.shape
    w = f64(np.asarray(w, np.float32).astype(ml_dtypes.bfloat16)).reshape(k // 32, 32, n)
    amax = np.abs(w).max(1)
    if fmt == "e4m3":
        byte = np.frexp(amax)[1] - 1 + 127 - 7
    else:
        mant, ex = np.frexp(amax / 6.0)
        byte = np.where(mant > 0.5, ex, ex - 1) + 127
    byte = np.clip(np.where(amax > 0, byte, 1), 1, 254)
    scaled = (w * np.exp2(127.0 - byte)[:, None, :]).reshape(k, n).astype(np.float32)
    by_word = np.ascontiguousarray(scaled.reshape(k // 512, 128, 4, n).transpose(0, 1, 3, 2))
    if fmt == "e4m3":
        words = by_word.astype(ml_dtypes.float8_e4m3fn).view(np.uint8)
    else:
        c = by_word.astype(ml_dtypes.float4_e2m1fn).view(np.uint8) & 0xF
        words = (c[..., 0::2] | (c[..., 1::2] << 4)).reshape(k // 512, 128, 2 * n)
    return np.ascontiguousarray(words), np.ascontiguousarray(byte.astype(np.uint8).reshape(k // 512, 16, n))


def unpack_weight(words, scales, fmt):
    g, _, n = scales.shape
    words = np.ascontiguousarray(words).reshape(g, 128, n, -1)
    if fmt == "e4m3":
        vals = words.view(ml_dtypes.float8_e4m3fn).astype(np.float64)
    else:
        nib = np.empty((g, 128, n, 4), np.uint8)
        nib[..., 0::2] = words & 0xF
        nib[..., 1::2] = words >> 4
        vals = E2M1[nib]
    vals = vals * np.repeat(np.exp2(scales.astype(np.float64) - 127.0), 8, axis=1)[..., None]
    return vals.transpose(0, 1, 3, 2).reshape(g * 512, n)


def gelu(v):
    return 0.5 * v * (1.0 + np.tanh(np.sqrt(2.0 / np.pi) * (v + 0.044715 * v**3)))


K, T, S, H, T2, P = 1536, 2048, 512, 1024, 1024, 512


def setup_inputs():
    n = np.random.standard_normal
    s = mx_kscale(K)[:, None]
    u = mx_kscale(H)[:, None]
    d = {}
    d["tab_words"], d["tab_scales"] = pack_weight(n((K, T)) * s, "e4m3")
    d["wa"] = (1.8 * n((K, H)) / K**0.5 / s * u.T).astype(np.float32)
    d["wb_words"], d["wb_scales"] = pack_weight(1.5 * n((K, H)) / K**0.5 / s, "e2m1")
    d["wgs"] = np.exp(0.3 * n((128, S))).astype(np.float32)
    d["page0"] = (n((H, T2)) * u).astype(np.float32)
    d["cen"] = (0.8 * n(H) * u[:, 0]).astype(np.float32)
    d["gv"] = (n(H) / H**0.5 / u[:, 0]**2).astype(np.float32)
    d["sv"] = (0.8 * np.exp(0.6 * n(T2))).astype(np.float32)
    d["offs"] = striped(np.random.permutation(T)[:S])
    d["offs2"] = striped(np.random.permutation(T2)[:S])
    d["offs3"] = striped(np.random.permutation(T2)[:P])
    return d


def reference(tab_words, tab_scales, wa, wb_words, wb_scales, wgs, page0, cen, gv, sv, offs, offs2, offs3):
    v = unpack_weight(tab_words, tab_scales, "e4m3")[:, unstriped(offs)]
    wb = unpack_weight(wb_words, wb_scales, "e2m1")
    a = mxq(f64(wa), 0, "e4m3").T @ v
    b = wb.T @ v
    h = a * np.exp(-np.abs(b))
    page = f64(page0).copy()
    page[:, unstriped(offs2)] = np.tile(f64(wgs), (H // 128, 1)) * h
    x = (page[:, unstriped(offs3)] - f64(cen)[:, None]) * f64(gv)[:, None]
    e = mxq(page, 0, "e4m3").T @ mxq(x, 0, "e4m3")
    return np.sqrt(np.square(e) + f64(sv)[:, None])

@@ -1,0 +1,369 @@
+from contextlib import ExitStack
+
+import concourse.mybir as mybir
+from concourse.masks import make_identity
+
+F32 = mybir.dt.float32
+BF16 = mybir.dt.bfloat16
+I32 = mybir.dt.int32
+U32 = mybir.dt.uint32
+U16 = mybir.dt.uint16
+U8 = mybir.dt.uint8
+FP8X4 = mybir.dt.float8_e4m3fn_x4
+FP4X4 = mybir.dt.float4_e2m1fn_x4
+ACT = mybir.ActivationFunctionType
+ALU = mybir.AluOpType
+
+K, T, S, H, T2, NP = 1536, 2048, 512, 1024, 1024, 512
+P = 128
+KP = K // 512
+HP = H // 512
+FLOPS = 2 * 2 * K * H * S + 2 * H * T2 * NP
+
+
+def tile_list_hide_slot_scores_kernel(
+    tc, tab_words, tab_scales, wa, wb_words, wb_scales, wgs, page0, cen, gv, sv, offs, offs2, offs3, out
+):
+    nc = tc.nc
+    with ExitStack() as ctx:
+        keep = ctx.enter_context(tc.tile_pool(name="keep", bufs=1))
+        work = ctx.enter_context(tc.tile_pool(name="work", bufs=1))
+        psum = ctx.enter_context(tc.psum_pool(name="psum", bufs=1))
+
+        def bank(k, name):
+            return psum.tile([P, 512], F32, name=name, tag="bank%d" % k)
+
+        def big(shape, dtype, name):
+            return work.tile(shape, dtype, name=name, tag="big", bufs=5, align_bytes=64)
+
+        def row(name):
+            return work.tile([P, 512], F32, name=name, tag="row", bufs=8, align_bytes=64)
+
+        list1 = keep.tile([P, S // 16], U16, name="list1")
+        list2 = keep.tile([P, S // 16], U16, name="list2")
+        list3 = keep.tile([P, NP // 16], U16, name="list3")
+
+        tab_sc = work.tile([P, KP * T], U8, name="tab_sc", tag="tab_sc", align_bytes=64)
+        wb_sc_raw = keep.tile([P, KP, H], U8, name="wb_sc_raw", align_bytes=64)
+        vec_rows = keep.tile([P, P], F32, name="vec_rows")
+        ident = keep.tile([P, P], F32, name="ident")
+        warm = keep.tile([P, 2], F32, name="warm")
+        nc.vector.memset(tab_sc[:].bitcast(I32), 0)
+        nc.vector.memset(wb_sc_raw[:].rearrange("p a c -> p (a c)").bitcast(I32), 0)
+        make_identity(nc, ident[:])
+        nc.vector.memset(vec_rows[:], 0.0)
+        nc.scalar.activation(warm[:, 0:1], vec_rows[:, 0:1], ACT.Exp)
+
+        wa_raw = {}
+
+        def load_wa(a, b, parts=1):
+            wa_raw[a, b] = big([P, 4, 512], F32, "wa_raw%d%d" % (a, b))
+            rows = wa[512 * a : 512 * (a + 1), 512 * b : 512 * (b + 1)].rearrange("(p j) c -> p j c", j=4)
+            for k in range(parts):
+                part = slice(4 * k // parts, 4 * (k + 1) // parts)
+                nc.sync.dma_start(out=wa_raw[a, b][:, part, :], in_=rows[:, part, :])
+
+        wb_raw = [keep.tile([P, KP, 256], I32, name="wb_raw%d" % b, align_bytes=64) for b in range(HP)]
+
+        def load_wb(b):
+            nc.sync.dma_start(
+                out=wb_raw[b][:],
+                in_=wb_words[:, :, 1024 * b : 1024 * (b + 1)].bitcast(I32).rearrange("a p w -> p a w"),
+            )
+
+        page = [keep.tile([P, T2], F32, name="page%d" % s, align_bytes=64) for s in range(8)]
+
+        def load_page(s):
+            b, t = divmod(s, 4)
+            rows = page0[512 * b : 512 * (b + 1), :].rearrange("(g t i) m -> t g i m", t=4, i=8)
+            nc.sync.dma_start(out=page[s][:], in_=rows[t])
+
+        tab_w = [big([P, T], I32, "tab_w%d" % a) for a in range(KP - 1)]
+        tab_w.append(work.tile([P, T], I32, name="tab_w2", tag="wa_g2", align_bytes=64))
+
+        def load_tab(a):
+            nc.sync.dma_start(out=tab_w[a][:], in_=tab_words[a].rearrange("p n t -> p (n t)").bitcast(I32))
+
+        wgs_sb = keep.tile([P, S], F32, name="wgs_sb")
+        nc.sync.dma_start(list1[:], offs)
+        nc.sync.dma_start(list2[:], offs2)
+        nc.sync.dma_start(list3[:], offs3)
+        nc.sync.dma_start(out=wgs_sb[:], in_=wgs)
+        load_wa(0, 0, 4)
+        for q in range(4):
+            nc.sync.dma_start(
+                out=tab_sc[32 * q : 32 * q + 4, :].bitcast(I32),
+                in_=tab_scales[:, 4 * q : 4 * q + 4, :].bitcast(I32).rearrange("a r w -> r a w"),
+            )
+        load_tab(0)
+        load_wb(0)
+        load_wa(1, 0)
+        for q in range(4):
+            nc.sync.dma_start(
+                out=wb_sc_raw[32 * q : 32 * q + 4].rearrange("p a c -> p (a c)").bitcast(I32),
+                in_=wb_scales[:, 4 * q : 4 * q + 4, :].bitcast(I32).rearrange("a r w -> r a w"),
+            )
+        load_tab(1)
+        load_tab(2)
+        load_wa(2, 0)
+        load_wb(1)
+        load_page(0)
+        for b in range(HP):
+            for k, vec in enumerate((cen, gv)):
+                nc.sync.dma_start(
+                    out=vec_rows[8 * k + 4 * b : 8 * k + 4 * b + 4, :],
+                    in_=vec[512 * b : 512 * (b + 1)].rearrange("(g t i) -> t g i", t=4, i=8),
+                )
+        nc.sync.dma_start(out=vec_rows[16:24, :], in_=sv.rearrange("(c p) -> c p", p=P))
+        load_page(1)
+        load_wa(0, 1)
+        load_wa(1, 1)
+        load_page(2)
+        load_wa(2, 1)
+        for s in (3, 4, 5, 6, 7):
+            load_page(s)
+
+        v_sc_all = keep.tile([P, KP, S], U8, name="v_sc_all", align_bytes=64)
+        for a in range(KP):
+            nc.vector.tensor_copy(v_sc_all[:, a, :], tab_sc[:, T * a : T * (a + 1)].indirect(list1[:]))
+        v_sc = [v_sc_all[:, a, :] for a in range(KP)]
+        v_w_all = work.tile([P, KP, S], U32, name="v_w_all", tag="tab_sc", align_bytes=64)
+        v_w = [v_w_all[:, a, :] for a in range(KP)]
+        for a in range(KP):
+            nc.vector.tensor_copy(v_w[a], tab_w[a][:].bitcast(U32).indirect(list1[:]))
+
+        wb_sc = keep.tile([P, KP * HP, 512], U8, name="wb_sc", align_bytes=64)
+        nc.vector.tensor_copy(
+            wb_sc[:].bitcast(I32).rearrange("p c (t g w) -> p c t g w", t=4, w=2),
+            wb_sc_raw[:].rearrange("p a (b c) -> p (a b) c", b=HP).bitcast(I32).rearrange(
+                "p c (g t w) -> p c t g w", t=4, w=2
+            ),
+        )
+        wb_w = [keep.tile([P, KP, 1024], U8, name="wb_w%d" % b, align_bytes=64) for b in range(HP)]
+
+        def deal_wb(b):
+            nc.vector.tensor_copy(
+                wb_w[b][:].bitcast(I32).rearrange("p a (t g w) -> p a t g w", t=4, w=4),
+                wb_raw[b][:].rearrange("p a (g t w) -> p a t g w", t=4, w=4),
+            )
+
+        wa_w = {}
+        wa_sc = {}
+        wa_g = {}
+
+        def quantise_wa(a, b, copy, by_slot):
+            tag = "wa_g%d" % a
+            grouped = work.tile([P, 4, 512], BF16, name="wa_g%d%d" % (a, b), tag=tag, align_bytes=64)
+            wa_g[a, b] = grouped
+            wa_w[a, b] = keep.tile([P, 512], U32, name="wa_w%d%d" % (a, b), align_bytes=64)
+            wa_sc[a, b] = keep.tile([P, 512], U8, name="wa_sc%d%d" % (a, b), align_bytes=64)
+            src = wa_raw[a, b][:].rearrange("p j (g t i) -> p t g i j", t=4, i=8)
+            dst = grouped[:].rearrange("p t (g i j) -> p t g i j", i=8, j=4)
+            if not by_slot:
+                copy(dst, src)
+                nc.vector.quantize_mx(
+                    wa_w[a, b][:].bitcast(FP8X4), wa_sc[a, b][:], grouped[:].rearrange("p t c -> p (t c)")
+                )
+                return None
+
+            def slots(first, last, slot_copy):
+                for t in range(first, last):
+                    slot_copy(dst[:, t], src[:, t])
+                for t in range(first, last):
+                    cols = slice(P * t, P * (t + 1))
+                    nc.vector.quantize_mx(wa_w[a, b][:, cols].bitcast(FP8X4), wa_sc[a, b][:, cols], grouped[:, t, :])
+
+            return slots
+
+        quantise_wa(0, 0, nc.scalar.copy, False)
+        deal_wb(0)
+
+        wgs_t_ps = bank(7, "wgs_t_ps")
+        for c in range(4):
+            nc.tensor.transpose(wgs_t_ps[:, P * c : P * (c + 1)], wgs_sb[:, P * c : P * (c + 1)], ident[:])
+        wgs_t = work.tile([P, 4, 4, P], F32, name="wgs_t", tag="il", align_bytes=64)
+        wgs_dealt = keep.tile([P, 4, S], F32, name="wgs_dealt", align_bytes=64)
+        for t in range(4):
+            src = wgs_t_ps[:].rearrange("p (c g t i) -> p t c g i", c=4, t=4, i=8)[:, t]
+            nc.scalar.copy(
+                wgs_t[:, t].rearrange("p c (q g i) -> p c q g i", q=4, i=8),
+                src.unsqueeze(2).broadcast_to([P, 4, 4, 4, 8]),
+            )
+        for t in range(4):
+            back = bank(t, "wgs_back%d" % t)
+            for c in range(4):
+                nc.tensor.transpose(back[:, P * c : P * (c + 1)], wgs_t[:, t, c, :], ident[:])
+            nc.scalar.copy(wgs_dealt[:, t, :], back[:])
+
+        quantise_wa(1, 0, nc.scalar.copy, False)
+
+        damp = {}
+        sizes = keep.tile([P, 2, S], F32, name="sizes", align_bytes=64)
+
+        def make_damp(s):
+            b, t = divmod(s, 4)
+            acc = bank(4 + t, "b%d" % s)
+            for a in range(KP):
+                nc.tensor.matmul_mx(
+                    acc[:],
+                    lhsT=wb_w[b][:, a, 256 * t : 256 * (t + 1)].bitcast(FP4X4),
+                    lhsT_scale=wb_sc[:, HP * a + b, P * t : P * (t + 1)],
+                    rhs=v_w[a].bitcast(FP8X4),
+                    rhs_scale=v_sc[a],
+                    start=(a == 0),
+                    stop=(a == KP - 1),
+                )
+            size = sizes[:, s % 2, :]
+            nc.scalar.activation(size, acc[:], ACT.Abs)
+            damp[s] = row("damp%d" % s)
+            nc.scalar.activation(damp[s][:], size, ACT.Exp, scale=-1.0)
+
+        feat = {}
+
+        def make_feat(s, home):
+            b, t = divmod(s, 4)
+            acc = bank(t, "a%d" % s)
+            for a in range(KP):
+                nc.tensor.matmul_mx(
+                    acc[:],
+                    lhsT=wa_w[a, b][:, P * t : P * (t + 1)].bitcast(FP8X4),
+                    lhsT_scale=wa_sc[a, b][:, P * t : P * (t + 1)],
+                    rhs=v_w[a].bitcast(FP8X4),
+                    rhs_scale=v_sc[a],
+                    start=(a == 0),
+                    stop=(a == KP - 1),
+                )
+            feat[s] = home
+            nc.vector.tensor_tensor(home, acc[:], damp[s][:], ALU.mult)
+
+        staged = {}
+        picked = {}
+
+        def put(s):
+            b, t = divmod(s, 4)
+            nc.vector.tensor_tensor(page[s][:].indirect(list2[:]), feat[s], wgs_dealt[:, t, :], ALU.mult)
+            if s < 7:
+                if t == 0:
+                    staged[b] = keep.tile([P, 4 - b, T2], F32, name="staged%d" % b, align_bytes=64)
+                nc.sync.dma_start(out=staged[b][:, t, :], in_=page[s][:])
+
+        def fetch(s):
+            picked[s] = keep.tile([P, NP], F32, name="picked%d" % s, align_bytes=64)[:]
+            nc.vector.tensor_copy(picked[s], page[s][:].indirect(list3[:]))
+
+        def centre(s, x_il):
+            t = s % 4
+            if s < 6:
+                nc.scalar.activation(
+                    x_il[:, :, t], picked[s], ACT.Identity, bias=shift[:, s : s + 1], scale=vecs[:, 8 + s : 9 + s]
+                )
+            else:
+                nc.vector.tensor_scalar(
+                    x_il[:, :, t], picked[s], vecs[:, s : s + 1], vecs[:, 8 + s : 9 + s], ALU.subtract, ALU.mult
+                )
+
+        x_w = [keep.tile([P, NP], U32, name="x_w%d" % b, align_bytes=64) for b in range(HP)]
+        x_sc = [keep.tile([P, NP], U8, name="x_sc%d" % b, align_bytes=64) for b in range(HP)]
+        pg_w = [keep.tile([P, T2], U32, name="pg_w%d" % b, align_bytes=64) for b in range(HP)]
+        pg_sc = [keep.tile([P, T2], U8, name="pg_sc%d" % b, align_bytes=64) for b in range(HP)]
+
+        def quantise_x(b, x_il):
+            nc.vector.quantize_mx(x_w[b][:].bitcast(FP8X4), x_sc[b][:], x_il.rearrange("p n t -> p (n t)"))
+
+        def quantise_page_cols(b, pg_il, cols):
+            nc.vector.quantize_mx(
+                pg_w[b][:, cols].bitcast(FP8X4), pg_sc[b][:, cols], pg_il[:, cols, :].rearrange("p m t -> p (m t)")
+            )
+
+        even = keep.tile([P, S], F32, name="feat_even", align_bytes=64)
+        first_odd = keep.tile([P, S], F32, name="feat_odd", align_bytes=64)
+        make_damp(0)
+        last_slots = quantise_wa(2, 0, None, True)
+        last_slots(0, 2, nc.vector.tensor_copy)
+        make_feat(0, even[:])
+        deal_wb(1)
+        put(0)
+        make_damp(1)
+        make_feat(1, first_odd[:])
+        last_slots(2, 4, nc.scalar.copy)
+        vec_ps = bank(4, "vec_ps")
+        nc.tensor.transpose(vec_ps[:, 0:P], vec_rows[:], ident[:])
+        vecs = keep.tile([P, 24], F32, name="vecs")
+        nc.scalar.copy(vecs[:], vec_ps[:, 0:24])
+        shift = keep.tile([P, 8], F32, name="shift")
+        nc.vector.scalar_tensor_tensor(shift[:], vecs[:, 0:8], -1.0, vecs[:, 8:16], ALU.mult, ALU.mult)
+
+
+        put(1)
+        make_damp(2)
+        make_feat(2, even[:])
+        fetch(0)
+        put(2)
+        make_damp(3)
+        for a in range(KP):
+            quantise_wa(a, 1, nc.scalar.copy, False)
+        for s in range(4, 8):
+            make_damp(s)
+        nc.scalar.activation(warm[:, 1:2], damp[7][:, 0:1], ACT.Sqrt)
+        odd = wa_g[2, 1][:, 0:2, :].rearrange("p t c -> p (t c)").bitcast(F32)
+        for s in range(3, 7):
+            make_feat(s, odd if s % 2 else even[:])
+            fetch(s - 2)
+            put(s)
+        fetch(5)
+        x_il = sizes[:].rearrange("p h n -> p (h n)").bitcast(BF16).rearrange("p (n t) -> p n t", t=4)
+        for s in range(3):
+            centre(s, x_il)
+        pg_il0 = work.tile([P, T2, 4], BF16, name="pg_il0", tag="il", align_bytes=64)
+        for c in range(2):
+            cols = slice(512 * c, 512 * (c + 1))
+            nc.scalar.copy(pg_il0[:, cols, :], staged[0][:, :, cols].rearrange("p t m -> p m t"))
+        centre(3, x_il)
+        quantise_x(0, x_il)
+        for c in range(2):
+            quantise_page_cols(0, pg_il0, slice(512 * c, 512 * (c + 1)))
+        spent = staged[0][:].rearrange("p t m -> p (t m)").bitcast(BF16)
+        x_il = spent[:, 4096:6144].rearrange("p (n t) -> p n t", t=4)
+        centre(4, x_il)
+        centre(5, x_il)
+        make_feat(7, pg_il0[:].rearrange("p m t -> p (m t)").bitcast(F32)[:, 1024:1536])
+        fetch(6)
+        centre(6, x_il)
+        score = [bank(m, "score%d" % m) for m in range(8)]
+
+        def score_pass(m, b):
+            cols = slice(P * m, P * (m + 1))
+            nc.tensor.matmul_mx(
+                score[m][:],
+                lhsT=pg_w[b][:, cols].bitcast(FP8X4),
+                lhsT_scale=pg_sc[b][:, cols],
+                rhs=x_w[b][:].bitcast(FP8X4),
+                rhs_scale=x_sc[b][:],
+                start=(b == 0),
+                stop=(b == HP - 1),
+            )
+
+        for m in range(8):
+            score_pass(m, 0)
+        pg_il1 = spent[:, 0:4096].rearrange("p (m t) -> p m t", t=4)
+        nc.scalar.copy(pg_il1[:, :, 0:3], staged[1][:].rearrange("p t m -> p m t"))
+        put(7)
+        fetch(7)
+        centre(7, x_il)
+        for c in range(4):
+            cols = slice(256 * c, 256 * (c + 1))
+            nc.scalar.copy(pg_il1[:, cols, 3], page[7][:, cols])
+            quantise_page_cols(1, pg_il1, cols)
+            if c == 0:
+                quantise_x(1, x_il)
+
+        for m in range(8):
+            score_pass(m, 1)
+            res = row("res%d" % m)
+            if m in (0, 2, 4):
+                nc.scalar.activation(res[:], score[m][:], ACT.Square)
+            else:
+                nc.vector.tensor_copy(res[:], score[m][:])
+                nc.vector.tensor_tensor(res[:], score[m][:], res[:], ALU.mult)
+            nc.scalar.activation(res[:], res[:], ACT.Sqrt, bias=vecs[:, 16 + m : 17 + m])
+            nc.sync.dma_start(out=out[P * m : P * (m + 1), :], in_=res[:])

@@ -34,7 +34,7 @@ def tile_list_hide_slot_scores_kernel(
             return psum.tile([P, 512], F32, name=name, tag="bank%d" % k)
 
         def big(shape, dtype, name):
-            return work.tile(shape, dtype, name=name, tag="big", bufs=5, align_bytes=64)
+            return work.tile(shape, dtype, name=name, tag="big", bufs=6, align_bytes=64)
 
         def row(name):
             return work.tile([P, 512], F32, name=name, tag="row", bufs=8, align_bytes=64)
@@ -50,14 +50,17 @@ def tile_list_hide_slot_scores_kernel(
         warm = keep.tile([P, 2], F32, name="warm")
         nc.vector.memset(tab_sc[:].bitcast(I32), 0)
         nc.vector.memset(wb_sc_raw[:].rearrange("p a c -> p (a c)").bitcast(I32), 0)
+        nc.gpsimd.memset(vec_rows[:], 0.0)
         make_identity(nc, ident[:])
-        nc.vector.memset(vec_rows[:], 0.0)
         nc.scalar.activation(warm[:, 0:1], vec_rows[:, 0:1], ACT.Exp)
 
         wa_raw = {}
 
         def load_wa(a, b, parts=1):
-            wa_raw[a, b] = big([P, 4, 512], F32, "wa_raw%d%d" % (a, b))
+            if (a, b) == (KP - 1, 0):
+                wa_raw[a, b] = work.tile([P, 4, 512], F32, name="wa_raw_last0", tag="late", align_bytes=64)
+            else:
+                wa_raw[a, b] = big([P, 4, 512], F32, "wa_raw%d%d" % (a, b))
             rows = wa[512 * a : 512 * (a + 1), 512 * b : 512 * (b + 1)].rearrange("(p j) c -> p j c", j=4)
             for k in range(parts):
                 part = slice(4 * k // parts, 4 * (k + 1) // parts)
@@ -78,13 +81,26 @@ def tile_list_hide_slot_scores_kernel(
             rows = page0[512 * b : 512 * (b + 1), :].rearrange("(g t i) m -> t g i m", t=4, i=8)
             nc.sync.dma_start(out=page[s][:], in_=rows[t])
 
-        tab_w = [big([P, T], I32, "tab_w%d" % a) for a in range(KP - 1)]
-        tab_w.append(work.tile([P, T], I32, name="tab_w2", tag="wa_g2", align_bytes=64))
+        tab_w = [big([P, T], I32, "tab_w%d" % a) for a in range(KP)]
 
         def load_tab(a):
             nc.sync.dma_start(out=tab_w[a][:], in_=tab_words[a].rearrange("p n t -> p (n t)").bitcast(I32))
 
         wgs_sb = keep.tile([P, S], F32, name="wgs_sb")
+
+        def load_wb_scales(q):
+            nc.sync.dma_start(
+                out=wb_sc_raw[32 * q : 32 * q + 4].rearrange("p a c -> p (a c)").bitcast(I32),
+                in_=wb_scales[:, 4 * q : 4 * q + 4, :].bitcast(I32).rearrange("a r w -> r a w"),
+            )
+
+        def load_by_slot(vec, first_row):
+            for b in range(HP):
+                nc.sync.dma_start(
+                    out=vec_rows[first_row + 4 * b : first_row + 4 * b + 4, :],
+                    in_=vec[512 * b : 512 * (b + 1)].rearrange("(g t i) -> t g i", t=4, i=8),
+                )
+
         nc.sync.dma_start(list1[:], offs)
         nc.sync.dma_start(list2[:], offs2)
         nc.sync.dma_start(list3[:], offs3)
@@ -97,24 +113,17 @@ def tile_list_hide_slot_scores_kernel(
             )
         load_tab(0)
         load_wb(0)
+        load_by_slot(cen, 0)
         load_wa(1, 0)
-        for q in range(4):
-            nc.sync.dma_start(
-                out=wb_sc_raw[32 * q : 32 * q + 4].rearrange("p a c -> p (a c)").bitcast(I32),
-                in_=wb_scales[:, 4 * q : 4 * q + 4, :].bitcast(I32).rearrange("a r w -> r a w"),
-            )
+        load_by_slot(gv, 8)
+        nc.sync.dma_start(out=vec_rows[16:24, :], in_=sv.rearrange("(c p) -> c p", p=P))
         load_tab(1)
+        for q in range(4):
+            load_wb_scales(q)
         load_tab(2)
         load_wa(2, 0)
-        load_wb(1)
         load_page(0)
-        for b in range(HP):
-            for k, vec in enumerate((cen, gv)):
-                nc.sync.dma_start(
-                    out=vec_rows[8 * k + 4 * b : 8 * k + 4 * b + 4, :],
-                    in_=vec[512 * b : 512 * (b + 1)].rearrange("(g t i) -> t g i", t=4, i=8),
-                )
-        nc.sync.dma_start(out=vec_rows[16:24, :], in_=sv.rearrange("(c p) -> c p", p=P))
+        load_wb(1)
         load_page(1)
         load_wa(0, 1)
         load_wa(1, 1)
@@ -139,44 +148,43 @@ def tile_list_hide_slot_scores_kernel(
                 "p c (g t w) -> p c t g w", t=4, w=2
             ),
         )
-        wb_w = [keep.tile([P, KP, 1024], U8, name="wb_w%d" % b, align_bytes=64) for b in range(HP)]
+        wb_w = {}
 
-        def deal_wb(b):
+        def deal_wb(b, home):
+            wb_w[b] = home
             nc.vector.tensor_copy(
-                wb_w[b][:].bitcast(I32).rearrange("p a (t g w) -> p a t g w", t=4, w=4),
+                home.bitcast(I32).rearrange("p a (t g w) -> p a t g w", t=4, w=4),
                 wb_raw[b][:].rearrange("p a (g t w) -> p a t g w", t=4, w=4),
             )
 
         wa_w = {}
         wa_sc = {}
-        wa_g = {}
+        sizes = keep.tile([P, 4, S], F32, name="sizes", align_bytes=64)
 
-        def quantise_wa(a, b, copy, by_slot):
-            tag = "wa_g%d" % a
-            grouped = work.tile([P, 4, 512], BF16, name="wa_g%d%d" % (a, b), tag=tag, align_bytes=64)
-            wa_g[a, b] = grouped
+        def quantise_wa(a, b, grouped, copy, parts):
             wa_w[a, b] = keep.tile([P, 512], U32, name="wa_w%d%d" % (a, b), align_bytes=64)
             wa_sc[a, b] = keep.tile([P, 512], U8, name="wa_sc%d%d" % (a, b), align_bytes=64)
             src = wa_raw[a, b][:].rearrange("p j (g t i) -> p t g i j", t=4, i=8)
-            dst = grouped[:].rearrange("p t (g i j) -> p t g i j", i=8, j=4)
-            if not by_slot:
-                copy(dst, src)
-                nc.vector.quantize_mx(
-                    wa_w[a, b][:].bitcast(FP8X4), wa_sc[a, b][:], grouped[:].rearrange("p t c -> p (t c)")
-                )
-                return None
+            dst = grouped.rearrange("p (t g i j) -> p t g i j", t=4, i=8, j=4)
+            step = 4 // parts
+            for k in range(parts + 1):
+                if k < parts:
+                    copy(dst[:, step * k : step * (k + 1)], src[:, step * k : step * (k + 1)])
+                if k > 0:
+                    cols = slice(P * step * (k - 1), P * step * k)
+                    nc.vector.quantize_mx(
+                        wa_w[a, b][:, cols].bitcast(FP8X4),
+                        wa_sc[a, b][:, cols],
+                        grouped[:, 4 * cols.start : 4 * cols.stop],
+                    )
 
-            def slots(first, last, slot_copy):
-                for t in range(first, last):
-                    slot_copy(dst[:, t], src[:, t])
-                for t in range(first, last):
-                    cols = slice(P * t, P * (t + 1))
-                    nc.vector.quantize_mx(wa_w[a, b][:, cols].bitcast(FP8X4), wa_sc[a, b][:, cols], grouped[:, t, :])
+        group = keep.tile([P, 2048], BF16, name="group", align_bytes=64)
 
-            return slots
+        def spent_raw(a, b, dtype):
+            return wa_raw[a, b][:].rearrange("p j c -> p (j c)").bitcast(dtype)
 
-        quantise_wa(0, 0, nc.scalar.copy, False)
-        deal_wb(0)
+        quantise_wa(0, 0, group[:], nc.scalar.copy, 1)
+        deal_wb(0, keep.tile([P, KP, 1024], U8, name="wb_w0", align_bytes=64)[:])
 
         wgs_t_ps = bank(7, "wgs_t_ps")
         for c in range(4):
@@ -195,14 +203,21 @@ def tile_list_hide_slot_scores_kernel(
                 nc.tensor.transpose(back[:, P * c : P * (c + 1)], wgs_t[:, t, c, :], ident[:])
             nc.scalar.copy(wgs_dealt[:, t, :], back[:])
 
-        quantise_wa(1, 0, nc.scalar.copy, False)
+        vec_ps = bank(6, "vec_ps")
+        nc.tensor.transpose(vec_ps[:, 0:P], vec_rows[:], ident[:])
+        vecs = keep.tile([P, 24], F32, name="vecs")
+        nc.scalar.copy(vecs[:], vec_ps[:, 0:24])
+        shift = keep.tile([P, 8], F32, name="shift")
+        nc.vector.scalar_tensor_tensor(shift[:], vecs[:, 0:8], -1.0, vecs[:, 8:16], ALU.mult, ALU.mult)
+
+
+        quantise_wa(1, 0, group[:], nc.scalar.copy, 1)
 
         damp = {}
-        sizes = keep.tile([P, 2, S], F32, name="sizes", align_bytes=64)
 
         def make_damp(s):
             b, t = divmod(s, 4)
-            acc = bank(4 + t, "b%d" % s)
+            acc = bank((4, 5, 4, 5, 6, 7, 4, 5)[s], "b%d" % s)
             for a in range(KP):
                 nc.tensor.matmul_mx(
                     acc[:],
@@ -213,7 +228,7 @@ def tile_list_hide_slot_scores_kernel(
                     start=(a == 0),
                     stop=(a == KP - 1),
                 )
-            size = sizes[:, s % 2, :]
+            size = sizes[:, 2 * b + s % 2, :]
             nc.scalar.activation(size, acc[:], ACT.Abs)
             damp[s] = row("damp%d" % s)
             nc.scalar.activation(damp[s][:], size, ACT.Exp, scale=-1.0)
@@ -222,7 +237,7 @@ def tile_list_hide_slot_scores_kernel(
 
         def make_feat(s, home):
             b, t = divmod(s, 4)
-            acc = bank(t, "a%d" % s)
+            acc = bank(s % 2, "a%d" % s)
             for a in range(KP):
                 nc.tensor.matmul_mx(
                     acc[:],
@@ -247,8 +262,10 @@ def tile_list_hide_slot_scores_kernel(
                     staged[b] = keep.tile([P, 4 - b, T2], F32, name="staged%d" % b, align_bytes=64)
                 nc.sync.dma_start(out=staged[b][:, t, :], in_=page[s][:])
 
-        def fetch(s):
-            picked[s] = keep.tile([P, NP], F32, name="picked%d" % s, align_bytes=64)[:]
+        def fetch(s, home=None):
+            if home is None:
+                home = keep.tile([P, NP], F32, name="picked%d" % s, align_bytes=64)[:]
+            picked[s] = home
             nc.vector.tensor_copy(picked[s], page[s][:].indirect(list3[:]))
 
         def centre(s, x_il):
@@ -278,40 +295,31 @@ def tile_list_hide_slot_scores_kernel(
         even = keep.tile([P, S], F32, name="feat_even", align_bytes=64)
         first_odd = keep.tile([P, S], F32, name="feat_odd", align_bytes=64)
         make_damp(0)
-        last_slots = quantise_wa(2, 0, None, True)
-        last_slots(0, 2, nc.vector.tensor_copy)
+        quantise_wa(2, 0, group[:], nc.vector.tensor_copy, 4)
         make_feat(0, even[:])
-        deal_wb(1)
+        deal_wb(1, work.tile([P, KP, 1024], U8, name="wb_w1", tag="late", align_bytes=64)[:])
         put(0)
         make_damp(1)
         make_feat(1, first_odd[:])
-        last_slots(2, 4, nc.scalar.copy)
-        vec_ps = bank(4, "vec_ps")
-        nc.tensor.transpose(vec_ps[:, 0:P], vec_rows[:], ident[:])
-        vecs = keep.tile([P, 24], F32, name="vecs")
-        nc.scalar.copy(vecs[:], vec_ps[:, 0:24])
-        shift = keep.tile([P, 8], F32, name="shift")
-        nc.vector.scalar_tensor_tensor(shift[:], vecs[:, 0:8], -1.0, vecs[:, 8:16], ALU.mult, ALU.mult)
-
-
+        fetch(0)
         put(1)
         make_damp(2)
         make_feat(2, even[:])
-        fetch(0)
+        fetch(1)
         put(2)
         make_damp(3)
-        for a in range(KP):
-            quantise_wa(a, 1, nc.scalar.copy, False)
+        quantise_wa(0, 1, sizes[:, 0:2, :].rearrange("p h n -> p (h n)").bitcast(BF16), nc.scalar.copy, 1)
+        quantise_wa(1, 1, spent_raw(0, 1, BF16)[:, 0:2048], nc.scalar.copy, 1)
+        quantise_wa(2, 1, spent_raw(1, 1, BF16)[:, 0:2048], nc.scalar.copy, 1)
         for s in range(4, 8):
             make_damp(s)
         nc.scalar.activation(warm[:, 1:2], damp[7][:, 0:1], ACT.Sqrt)
-        odd = wa_g[2, 1][:, 0:2, :].rearrange("p t c -> p (t c)").bitcast(F32)
+        odd = spent_raw(1, 1, F32)[:, 0:S]
         for s in range(3, 7):
             make_feat(s, odd if s % 2 else even[:])
-            fetch(s - 2)
+            fetch(s - 1, spent_raw(1, 1, F32)[:, S : 2 * S] if s == 3 else None)
             put(s)
-        fetch(5)
-        x_il = sizes[:].rearrange("p h n -> p (h n)").bitcast(BF16).rearrange("p (n t) -> p n t", t=4)
+        x_il = sizes[:, 2:4, :].rearrange("p h n -> p (h n)").bitcast(BF16).rearrange("p (n t) -> p n t", t=4)
         for s in range(3):
             centre(s, x_il)
         pg_il0 = work.tile([P, T2, 4], BF16, name="pg_il0", tag="il", align_bytes=64)

@@ -164,12 +164,13 @@ def tile_list_hide_slot_scores_kernel(
         def quantise_wa(a, b, grouped, copy, parts):
             wa_w[a, b] = keep.tile([P, 512], U32, name="wa_w%d%d" % (a, b), align_bytes=64)
             wa_sc[a, b] = keep.tile([P, 512], U8, name="wa_sc%d%d" % (a, b), align_bytes=64)
-            src = wa_raw[a, b][:].rearrange("p j (g t i) -> p t g i j", t=4, i=8)
-            dst = grouped.rearrange("p (t g i j) -> p t g i j", t=4, i=8, j=4)
+            src = wa_raw[a, b][:].rearrange("p j (g t h i) -> p t g h j i", t=4, h=2, i=4)
+            dst = grouped.rearrange("p (t g h i j) -> p t g h j i", t=4, h=2, i=4, j=4)
             step = 4 // parts
             for k in range(parts + 1):
                 if k < parts:
-                    copy(dst[:, step * k : step * (k + 1)], src[:, step * k : step * (k + 1)])
+                    for t in range(step * k, step * (k + 1)):
+                        copy(dst[:, t], src[:, t])
                 if k > 0:
                     cols = slice(P * step * (k - 1), P * step * k)
                     nc.vector.quantize_mx(
@@ -325,7 +326,10 @@ def tile_list_hide_slot_scores_kernel(
         pg_il0 = work.tile([P, T2, 4], BF16, name="pg_il0", tag="il", align_bytes=64)
         for c in range(2):
             cols = slice(512 * c, 512 * (c + 1))
-            nc.scalar.copy(pg_il0[:, cols, :], staged[0][:, :, cols].rearrange("p t m -> p m t"))
+            nc.scalar.copy(
+                pg_il0[:, cols, :].rearrange("p (c i) t -> p c t i", i=4),
+                staged[0][:, :, cols].rearrange("p t (c i) -> p c t i", i=4),
+            )
         centre(3, x_il)
         quantise_x(0, x_il)
         for c in range(2):
@@ -354,7 +358,10 @@ def tile_list_hide_slot_scores_kernel(
         for m in range(8):
             score_pass(m, 0)
         pg_il1 = spent[:, 0:4096].rearrange("p (m t) -> p m t", t=4)
-        nc.scalar.copy(pg_il1[:, :, 0:3], staged[1][:].rearrange("p t m -> p m t"))
+        nc.scalar.copy(
+            pg_il1[:, :, 0:3].rearrange("p (c i) t -> p c t i", i=4),
+            staged[1][:].rearrange("p t (c i) -> p c t i", i=4),
+        )
         put(7)
         fetch(7)
         centre(7, x_il)

from contextlib import ExitStack

import concourse.mybir as mybir
from concourse.masks import make_identity

F32 = mybir.dt.float32
BF16 = mybir.dt.bfloat16
I32 = mybir.dt.int32
U32 = mybir.dt.uint32
U16 = mybir.dt.uint16
U8 = mybir.dt.uint8
FP8X4 = mybir.dt.float8_e4m3fn_x4
FP4X4 = mybir.dt.float4_e2m1fn_x4
ACT = mybir.ActivationFunctionType
ALU = mybir.AluOpType

K, T, S, H, T2, NP = 1536, 2048, 512, 1024, 1024, 512
P = 128
KP = K // 512
HP = H // 512
FLOPS = 2 * 2 * K * H * S + 2 * H * T2 * NP


def tile_list_hide_slot_scores_kernel(
    tc, tab_words, tab_scales, wa, wb_words, wb_scales, wgs, page0, cen, gv, sv, offs, offs2, offs3, out
):
    nc = tc.nc
    with ExitStack() as ctx:
        keep = ctx.enter_context(tc.tile_pool(name="keep", bufs=1))
        work = ctx.enter_context(tc.tile_pool(name="work", bufs=1))
        psum = ctx.enter_context(tc.psum_pool(name="psum", bufs=1))

        def bank(k, name):
            return psum.tile([P, 512], F32, name=name, tag="bank%d" % k)

        def big(shape, dtype, name):
            return work.tile(shape, dtype, name=name, tag="big", bufs=6, align_bytes=64)

        def row(name):
            return work.tile([P, 512], F32, name=name, tag="row", bufs=8, align_bytes=64)

        list1 = keep.tile([P, S // 16], U16, name="list1")
        list2 = keep.tile([P, S // 16], U16, name="list2")
        list3 = keep.tile([P, NP // 16], U16, name="list3")

        tab_sc = work.tile([P, KP * T], U8, name="tab_sc", tag="tab_sc", align_bytes=64)
        wb_sc_raw = keep.tile([P, KP, H], U8, name="wb_sc_raw", align_bytes=64)
        vec_rows = keep.tile([P, P], F32, name="vec_rows")
        ident = keep.tile([P, P], F32, name="ident")
        warm = keep.tile([P, 2], F32, name="warm")
        nc.vector.memset(tab_sc[:].bitcast(I32), 0)
        nc.vector.memset(wb_sc_raw[:].rearrange("p a c -> p (a c)").bitcast(I32), 0)
        nc.gpsimd.memset(vec_rows[:], 0.0)
        make_identity(nc, ident[:])
        nc.scalar.activation(warm[:, 0:1], vec_rows[:, 0:1], ACT.Exp)

        wa_raw = {}

        def load_wa(a, b, parts=1):
            if (a, b) == (KP - 1, 0):
                wa_raw[a, b] = work.tile([P, 4, 512], F32, name="wa_raw_last0", tag="late", align_bytes=64)
            else:
                wa_raw[a, b] = big([P, 4, 512], F32, "wa_raw%d%d" % (a, b))
            rows = wa[512 * a : 512 * (a + 1), 512 * b : 512 * (b + 1)].rearrange("(p j) c -> p j c", j=4)
            for k in range(parts):
                part = slice(4 * k // parts, 4 * (k + 1) // parts)
                nc.sync.dma_start(out=wa_raw[a, b][:, part, :], in_=rows[:, part, :])

        wb_raw = [keep.tile([P, KP, 256], I32, name="wb_raw%d" % b, align_bytes=64) for b in range(HP)]

        def load_wb(b):
            nc.sync.dma_start(
                out=wb_raw[b][:],
                in_=wb_words[:, :, 1024 * b : 1024 * (b + 1)].bitcast(I32).rearrange("a p w -> p a w"),
            )

        page = [keep.tile([P, T2], F32, name="page%d" % s, align_bytes=64) for s in range(8)]

        def load_page(s):
            b, t = divmod(s, 4)
            rows = page0[512 * b : 512 * (b + 1), :].rearrange("(g t i) m -> t g i m", t=4, i=8)
            nc.sync.dma_start(out=page[s][:], in_=rows[t])

        tab_w = [big([P, T], I32, "tab_w%d" % a) for a in range(KP)]

        def load_tab(a):
            nc.sync.dma_start(out=tab_w[a][:], in_=tab_words[a].rearrange("p n t -> p (n t)").bitcast(I32))

        wgs_sb = keep.tile([P, S], F32, name="wgs_sb")

        def load_wb_scales(q):
            nc.sync.dma_start(
                out=wb_sc_raw[32 * q : 32 * q + 4].rearrange("p a c -> p (a c)").bitcast(I32),
                in_=wb_scales[:, 4 * q : 4 * q + 4, :].bitcast(I32).rearrange("a r w -> r a w"),
            )

        def load_by_slot(vec, first_row):
            for b in range(HP):
                nc.sync.dma_start(
                    out=vec_rows[first_row + 4 * b : first_row + 4 * b + 4, :],
                    in_=vec[512 * b : 512 * (b + 1)].rearrange("(g t i) -> t g i", t=4, i=8),
                )

        nc.sync.dma_start(list1[:], offs)
        nc.sync.dma_start(list2[:], offs2)
        nc.sync.dma_start(list3[:], offs3)
        nc.sync.dma_start(out=wgs_sb[:], in_=wgs)
        load_wa(0, 0, 4)
        for q in range(4):
            nc.sync.dma_start(
                out=tab_sc[32 * q : 32 * q + 4, :].bitcast(I32),
                in_=tab_scales[:, 4 * q : 4 * q + 4, :].bitcast(I32).rearrange("a r w -> r a w"),
            )
        load_tab(0)
        load_wb(0)
        load_by_slot(cen, 0)
        load_wa(1, 0)
        load_by_slot(gv, 8)
        nc.sync.dma_start(out=vec_rows[16:24, :], in_=sv.rearrange("(c p) -> c p", p=P))
        load_tab(1)
        for q in range(4):
            load_wb_scales(q)
        load_tab(2)
        load_wa(2, 0)
        load_page(0)
        load_wb(1)
        load_page(1)
        load_wa(0, 1)
        load_wa(1, 1)
        load_page(2)
        load_wa(2, 1)
        for s in (3, 4, 5, 6, 7):
            load_page(s)

        v_sc_all = keep.tile([P, KP, S], U8, name="v_sc_all", align_bytes=64)
        for a in range(KP):
            nc.vector.tensor_copy(v_sc_all[:, a, :], tab_sc[:, T * a : T * (a + 1)].indirect(list1[:]))
        v_sc = [v_sc_all[:, a, :] for a in range(KP)]
        v_w_all = work.tile([P, KP, S], U32, name="v_w_all", tag="tab_sc", align_bytes=64)
        v_w = [v_w_all[:, a, :] for a in range(KP)]
        for a in range(KP):
            nc.vector.tensor_copy(v_w[a], tab_w[a][:].bitcast(U32).indirect(list1[:]))

        wb_sc = keep.tile([P, KP * HP, 512], U8, name="wb_sc", align_bytes=64)
        nc.vector.tensor_copy(
            wb_sc[:].bitcast(I32).rearrange("p c (t g w) -> p c t g w", t=4, w=2),
            wb_sc_raw[:].rearrange("p a (b c) -> p (a b) c", b=HP).bitcast(I32).rearrange(
                "p c (g t w) -> p c t g w", t=4, w=2
            ),
        )
        wb_w = {}

        def deal_wb(b, home):
            wb_w[b] = home
            nc.vector.tensor_copy(
                home.bitcast(I32).rearrange("p a (t g w) -> p a t g w", t=4, w=4),
                wb_raw[b][:].rearrange("p a (g t w) -> p a t g w", t=4, w=4),
            )

        wa_w = {}
        wa_sc = {}
        sizes = keep.tile([P, 4, S], F32, name="sizes", align_bytes=64)

        def quantise_wa(a, b, grouped, copy, parts):
            wa_w[a, b] = keep.tile([P, 512], U32, name="wa_w%d%d" % (a, b), align_bytes=64)
            wa_sc[a, b] = keep.tile([P, 512], U8, name="wa_sc%d%d" % (a, b), align_bytes=64)
            src = wa_raw[a, b][:].rearrange("p j (g t h i) -> p t g h j i", t=4, h=2, i=4)
            dst = grouped.rearrange("p (t g h i j) -> p t g h j i", t=4, h=2, i=4, j=4)
            step = 4 // parts
            for k in range(parts + 1):
                if k < parts:
                    for t in range(step * k, step * (k + 1)):
                        copy(dst[:, t], src[:, t])
                if k > 0:
                    cols = slice(P * step * (k - 1), P * step * k)
                    nc.vector.quantize_mx(
                        wa_w[a, b][:, cols].bitcast(FP8X4),
                        wa_sc[a, b][:, cols],
                        grouped[:, 4 * cols.start : 4 * cols.stop],
                    )

        group = keep.tile([P, 2048], BF16, name="group", align_bytes=64)

        def spent_raw(a, b, dtype):
            return wa_raw[a, b][:].rearrange("p j c -> p (j c)").bitcast(dtype)

        quantise_wa(0, 0, group[:], nc.scalar.copy, 1)
        deal_wb(0, keep.tile([P, KP, 1024], U8, name="wb_w0", align_bytes=64)[:])

        wgs_t_ps = bank(7, "wgs_t_ps")
        for c in range(4):
            nc.tensor.transpose(wgs_t_ps[:, P * c : P * (c + 1)], wgs_sb[:, P * c : P * (c + 1)], ident[:])
        wgs_t = work.tile([P, 4, 4, P], F32, name="wgs_t", tag="il", align_bytes=64)
        wgs_dealt = keep.tile([P, 4, S], F32, name="wgs_dealt", align_bytes=64)
        for t in range(4):
            src = wgs_t_ps[:].rearrange("p (c g t i) -> p t c g i", c=4, t=4, i=8)[:, t]
            nc.scalar.copy(
                wgs_t[:, t].rearrange("p c (q g i) -> p c q g i", q=4, i=8),
                src.unsqueeze(2).broadcast_to([P, 4, 4, 4, 8]),
            )
        for t in range(4):
            back = bank(t, "wgs_back%d" % t)
            for c in range(4):
                nc.tensor.transpose(back[:, P * c : P * (c + 1)], wgs_t[:, t, c, :], ident[:])
            nc.scalar.copy(wgs_dealt[:, t, :], back[:])

        vec_ps = bank(6, "vec_ps")
        nc.tensor.transpose(vec_ps[:, 0:P], vec_rows[:], ident[:])
        vecs = keep.tile([P, 24], F32, name="vecs")
        nc.scalar.copy(vecs[:], vec_ps[:, 0:24])
        shift = keep.tile([P, 8], F32, name="shift")
        nc.vector.scalar_tensor_tensor(shift[:], vecs[:, 0:8], -1.0, vecs[:, 8:16], ALU.mult, ALU.mult)


        quantise_wa(1, 0, group[:], nc.scalar.copy, 1)

        damp = {}

        def make_damp(s):
            b, t = divmod(s, 4)
            acc = bank((4, 5, 4, 5, 6, 7, 4, 5)[s], "b%d" % s)
            for a in range(KP):
                nc.tensor.matmul_mx(
                    acc[:],
                    lhsT=wb_w[b][:, a, 256 * t : 256 * (t + 1)].bitcast(FP4X4),
                    lhsT_scale=wb_sc[:, HP * a + b, P * t : P * (t + 1)],
                    rhs=v_w[a].bitcast(FP8X4),
                    rhs_scale=v_sc[a],
                    start=(a == 0),
                    stop=(a == KP - 1),
                )
            size = sizes[:, 2 * b + s % 2, :]
            nc.scalar.activation(size, acc[:], ACT.Abs)
            damp[s] = row("damp%d" % s)
            nc.scalar.activation(damp[s][:], size, ACT.Exp, scale=-1.0)

        feat = {}

        def make_feat(s, home):
            b, t = divmod(s, 4)
            acc = bank(s % 2, "a%d" % s)
            for a in range(KP):
                nc.tensor.matmul_mx(
                    acc[:],
                    lhsT=wa_w[a, b][:, P * t : P * (t + 1)].bitcast(FP8X4),
                    lhsT_scale=wa_sc[a, b][:, P * t : P * (t + 1)],
                    rhs=v_w[a].bitcast(FP8X4),
                    rhs_scale=v_sc[a],
                    start=(a == 0),
                    stop=(a == KP - 1),
                )
            feat[s] = home
            nc.vector.tensor_tensor(home, acc[:], damp[s][:], ALU.mult)

        staged = {}
        picked = {}

        def put(s):
            b, t = divmod(s, 4)
            nc.vector.tensor_tensor(page[s][:].indirect(list2[:]), feat[s], wgs_dealt[:, t, :], ALU.mult)
            if s < 7:
                if t == 0:
                    staged[b] = keep.tile([P, 4 - b, T2], F32, name="staged%d" % b, align_bytes=64)
                nc.sync.dma_start(out=staged[b][:, t, :], in_=page[s][:])

        def fetch(s, home=None):
            if home is None:
                home = keep.tile([P, NP], F32, name="picked%d" % s, align_bytes=64)[:]
            picked[s] = home
            nc.vector.tensor_copy(picked[s], page[s][:].indirect(list3[:]))

        def centre(s, x_il):
            t = s % 4
            if s < 6:
                nc.scalar.activation(
                    x_il[:, :, t], picked[s], ACT.Identity, bias=shift[:, s : s + 1], scale=vecs[:, 8 + s : 9 + s]
                )
            else:
                nc.vector.tensor_scalar(
                    x_il[:, :, t], picked[s], vecs[:, s : s + 1], vecs[:, 8 + s : 9 + s], ALU.subtract, ALU.mult
                )

        x_w = [keep.tile([P, NP], U32, name="x_w%d" % b, align_bytes=64) for b in range(HP)]
        x_sc = [keep.tile([P, NP], U8, name="x_sc%d" % b, align_bytes=64) for b in range(HP)]
        pg_w = [keep.tile([P, T2], U32, name="pg_w%d" % b, align_bytes=64) for b in range(HP)]
        pg_sc = [keep.tile([P, T2], U8, name="pg_sc%d" % b, align_bytes=64) for b in range(HP)]

        def quantise_x(b, x_il):
            nc.vector.quantize_mx(x_w[b][:].bitcast(FP8X4), x_sc[b][:], x_il.rearrange("p n t -> p (n t)"))

        def quantise_page_cols(b, pg_il, cols):
            nc.vector.quantize_mx(
                pg_w[b][:, cols].bitcast(FP8X4), pg_sc[b][:, cols], pg_il[:, cols, :].rearrange("p m t -> p (m t)")
            )

        even = keep.tile([P, S], F32, name="feat_even", align_bytes=64)
        first_odd = keep.tile([P, S], F32, name="feat_odd", align_bytes=64)
        make_damp(0)
        quantise_wa(2, 0, group[:], nc.vector.tensor_copy, 4)
        make_feat(0, even[:])
        deal_wb(1, work.tile([P, KP, 1024], U8, name="wb_w1", tag="late", align_bytes=64)[:])
        put(0)
        make_damp(1)
        make_feat(1, first_odd[:])
        fetch(0)
        put(1)
        make_damp(2)
        make_feat(2, even[:])
        fetch(1)
        put(2)
        make_damp(3)
        quantise_wa(0, 1, sizes[:, 0:2, :].rearrange("p h n -> p (h n)").bitcast(BF16), nc.scalar.copy, 1)
        quantise_wa(1, 1, spent_raw(0, 1, BF16)[:, 0:2048], nc.scalar.copy, 1)
        quantise_wa(2, 1, spent_raw(1, 1, BF16)[:, 0:2048], nc.scalar.copy, 1)
        for s in range(4, 8):
            make_damp(s)
        nc.scalar.activation(warm[:, 1:2], damp[7][:, 0:1], ACT.Sqrt)
        odd = spent_raw(1, 1, F32)[:, 0:S]
        for s in range(3, 7):
            make_feat(s, odd if s % 2 else even[:])
            fetch(s - 1, spent_raw(1, 1, F32)[:, S : 2 * S] if s == 3 else None)
            put(s)
        x_il = sizes[:, 2:4, :].rearrange("p h n -> p (h n)").bitcast(BF16).rearrange("p (n t) -> p n t", t=4)
        for s in range(3):
            centre(s, x_il)
        pg_il0 = work.tile([P, T2, 4], BF16, name="pg_il0", tag="il", align_bytes=64)
        for c in range(2):
            cols = slice(512 * c, 512 * (c + 1))
            nc.scalar.copy(
                pg_il0[:, cols, :].rearrange("p (c i) t -> p c t i", i=4),
                staged[0][:, :, cols].rearrange("p t (c i) -> p c t i", i=4),
            )
        centre(3, x_il)
        quantise_x(0, x_il)
        for c in range(2):
            quantise_page_cols(0, pg_il0, slice(512 * c, 512 * (c + 1)))
        spent = staged[0][:].rearrange("p t m -> p (t m)").bitcast(BF16)
        x_il = spent[:, 4096:6144].rearrange("p (n t) -> p n t", t=4)
        centre(4, x_il)
        centre(5, x_il)
        make_feat(7, pg_il0[:].rearrange("p m t -> p (m t)").bitcast(F32)[:, 1024:1536])
        fetch(6)
        centre(6, x_il)
        score = [bank(m, "score%d" % m) for m in range(8)]

        def score_pass(m, b):
            cols = slice(P * m, P * (m + 1))
            nc.tensor.matmul_mx(
                score[m][:],
                lhsT=pg_w[b][:, cols].bitcast(FP8X4),
                lhsT_scale=pg_sc[b][:, cols],
                rhs=x_w[b][:].bitcast(FP8X4),
                rhs_scale=x_sc[b][:],
                start=(b == 0),
                stop=(b == HP - 1),
            )

        for m in range(8):
            score_pass(m, 0)
        pg_il1 = spent[:, 0:4096].rearrange("p (m t) -> p m t", t=4)
        nc.scalar.copy(
            pg_il1[:, :, 0:3].rearrange("p (c i) t -> p c t i", i=4),
            staged[1][:].rearrange("p t (c i) -> p c t i", i=4),
        )
        put(7)
        fetch(7)
        centre(7, x_il)
        for c in range(4):
            cols = slice(256 * c, 256 * (c + 1))
            nc.scalar.copy(pg_il1[:, cols, 3], page[7][:, cols])
            quantise_page_cols(1, pg_il1, cols)
            if c == 0:
                quantise_x(1, x_il)

        for m in range(8):
            score_pass(m, 1)
            res = row("res%d" % m)
            if m in (0, 2, 4):
                nc.scalar.activation(res[:], score[m][:], ACT.Square)
            else:
                nc.vector.tensor_copy(res[:], score[m][:])
                nc.vector.tensor_tensor(res[:], score[m][:], res[:], ALU.mult)
            nc.scalar.activation(res[:], res[:], ACT.Sqrt, bias=vecs[:, 16 + m : 17 + m])
            nc.sync.dma_start(out=out[P * m : P * (m + 1), :], in_=res[:])
